import numpy as np
import ml_dtypes


def mxq(x, axis, fmt="e4m3"):
    dtype, down = {"e4m3": (ml_dtypes.float8_e4m3fn, 7), "e5m2": (ml_dtypes.float8_e5m2, 14)}[fmt]
    v = np.moveaxis(np.asarray(x, np.float32).astype(ml_dtypes.bfloat16).astype(np.float64), axis, -1)
    blocks = v.reshape(v.shape[:-1] + (-1, 32))
    amax = np.abs(blocks).max(-1, keepdims=True)
    byte = np.maximum(np.where(amax > 0, np.frexp(amax)[1] - 1 + 127, 0) - down, 1)
    scale = np.exp2(byte - 127.0)
    codes = (blocks / scale).astype(np.float32).astype(dtype).astype(np.float64)
    return np.moveaxis((codes * scale).reshape(v.shape), -1, axis)


WIDE = False


def mx_kscale(k):
    if not WIDE:
        return np.ones(k)
    levels = np.array([10, -10, 5, -5, 0])
    if k % 512:
        return np.exp2(np.random.permutation(np.resize(levels, k // 32))).repeat(32)
    a = np.empty((k // 512, 16))
    for p in range(k // 512):
        a[p, :8] = np.random.permutation(np.resize(levels, 8))
        for g in range(8):
            far = levels[np.abs(levels - a[p, g]) >= 10]
            a[p, g + 8] = far[np.random.randint(len(far))]
    return np.exp2(a.ravel()).repeat(32)


def f64(x):
    return np.asarray(x).astype(np.float64)


def striped(idx):
    return np.tile(np.asarray(idx).reshape(-1, 16).T, (8, 1)).astype(np.uint16)


def unstriped(offs):
    return offs[:16].T.reshape(-1).astype(np.int64)


E2M1 = np.array([0.0, 0.5, 1.0, 1.5, 2.0, 3.0, 4.0, 6.0, -0.0, -0.5, -1.0, -1.5, -2.0, -3.0, -4.0, -6.0])


def pack_weight(w, fmt):
    k, n = w.shape
    w = f64(np.asarray(w, np.float32).astype(ml_dtypes.bfloat16)).reshape(k // 32, 32, n)
    amax = np.abs(w).max(1)
    if fmt == "e4m3":
        byte = np.frexp(amax)[1] - 1 + 127 - 7
    else:
        mant, ex = np.frexp(amax / 6.0)
        byte = np.where(mant > 0.5, ex, ex - 1) + 127
    byte = np.clip(np.where(amax > 0, byte, 1), 1, 254)
    scaled = (w * np.exp2(127.0 - byte)[:, None, :]).reshape(k, n).astype(np.float32)
    by_word = np.ascontiguousarray(scaled.reshape(k // 512, 128, 4, n).transpose(0, 1, 3, 2))
    if fmt == "e4m3":
        words = by_word.astype(ml_dtypes.float8_e4m3fn).view(np.uint8)
    else:
        c = by_word.astype(ml_dtypes.float4_e2m1fn).view(np.uint8) & 0xF
        words = (c[..., 0::2] | (c[..., 1::2] << 4)).reshape(k // 512, 128, 2 * n)
    return np.ascontiguousarray(words), np.ascontiguousarray(byte.astype(np.uint8).reshape(k // 512, 16, n))


def unpack_weight(words, scales, fmt):
    g, _, n = scales.shape
    words = np.ascontiguousarray(words).reshape(g, 128, n, -1)
    if fmt == "e4m3":
        vals = words.view(ml_dtypes.float8_e4m3fn).astype(np.float64)
    else:
        nib = np.empty((g, 128, n, 4), np.uint8)
        nib[..., 0::2] = words & 0xF
        nib[..., 1::2] = words >> 4
        vals = E2M1[nib]
    vals = vals * np.repeat(np.exp2(scales.astype(np.float64) - 127.0), 8, axis=1)[..., None]
    return vals.transpose(0, 1, 3, 2).reshape(g * 512, n)


K, R, F, T, J, M = 512, 128, 512, 2048, 512, 256


def setup_inputs():
    n = np.random.standard_normal
    idx = np.random.permutation(T)[:J]
    idx2 = np.random.permutation(J)[:M]
    idx3 = np.random.permutation(J)[:M]
    fk = mx_kscale(K)
    ff = mx_kscale(F)
    tabp = pack_weight(n((K, T)) / fk[:, None], "e4m3")
    return {
        "tab_words": tabp[0],
        "tab_scales": tabp[1],
        "w1": (n((K, R)) * 1 / np.sqrt(K) * fk[:, None]).astype(np.float32),
        "reserve": (np.random.uniform(0.3, 1.5, (R, 1))).astype(np.float32),
        "wo": (n((F, R)) * 1 / np.sqrt(F) * ff[:, None]).astype(np.float32),
        "dy": (n((F, M)) / ff[:, None]).astype(np.float32),
        "og": (np.random.uniform(0.3, 1.0, (R, 1))).astype(np.float32),
        "base": (0.3 * n((R, J))).astype(np.float32),
        "offs": striped(idx),
        "offs2": striped(idx2),
        "offs3": striped(idx3),
    }


def reference(tab_words, tab_scales, w1, reserve, wo, dy, og, base, offs, offs2, offs3):
    idx = unstriped(offs)
    idx2 = unstriped(offs2)
    idx3 = unstriped(offs3)
    tabu = unpack_weight(tab_words, tab_scales, "e4m3")
    w1q = mxq(f64(w1), 0, "e4m3")
    tabidxg = tabu[:, idx]
    a = w1q.T @ tabidxg
    h1 = np.exp(a)
    woq = mxq(f64(wo), 0, "e4m3")
    dyq = mxq(f64(dy), 0, "e4m3")
    c0 = woq.T @ dyq
    e1 = c0 / (h1[:, idx2] + h1[:, idx3] + f64(reserve))
    s1 = np.zeros((R, J))
    s1[:, idx2] = e1
    e2 = c0 * h1[:, idx2] / np.square(h1[:, idx2] + h1[:, idx3] + f64(reserve)) * (-1.0)
    s2 = np.zeros((R, J))
    s2[:, idx2] = e2
    e3 = c0 * h1[:, idx2] / np.square(h1[:, idx2] + h1[:, idx3] + f64(reserve)) * (-1.0)
    s3 = np.zeros((R, J))
    s3[:, idx3] = e3
    dh1 = s1 + s2 + s3
    da = dh1 * h1
    hda = da * 2.0
    hdh1 = hda * h1
    he3 = hdh1[:, idx3]
    he2 = hdh1[:, idx2]
    he1 = hdh1[:, idx2]
    e51 = he3 * (-1.0) / np.square(h1[:, idx2] + h1[:, idx3] + f64(reserve)) * c0
    s51 = np.zeros((R, J))
    s51[:, idx2] = e51
    e52 = he3 * (-1.0) * c0 * h1[:, idx2] / np.square(np.square(h1[:, idx2] + h1[:, idx3] + f64(reserve))) * (-1.0) * (h1[:, idx2] + h1[:, idx3] + f64(reserve)) * 2.0
    s52 = np.zeros((R, J))
    s52[:, idx2] = e52
    e53 = he2 * (-1.0) / np.square(h1[:, idx2] + h1[:, idx3] + f64(reserve)) * c0
    s53 = np.zeros((R, J))
    s53[:, idx2] = e53
    e54 = he2 * (-1.0) * c0 * h1[:, idx2] / np.square(np.square(h1[:, idx2] + h1[:, idx3] + f64(reserve))) * (-1.0) * (h1[:, idx2] + h1[:, idx3] + f64(reserve)) * 2.0
    s54 = np.zeros((R, J))
    s54[:, idx2] = e54
    e55 = he1 * c0 / np.square(h1[:, idx2] + h1[:, idx3] + f64(reserve)) * (-1.0)
    s55 = np.zeros((R, J))
    s55[:, idx2] = e55
    e56 = he3 * (-1.0) * c0 * h1[:, idx2] / np.square(np.square(h1[:, idx2] + h1[:, idx3] + f64(reserve))) * (-1.0) * (h1[:, idx2] + h1[:, idx3] + f64(reserve)) * 2.0
    s56 = np.zeros((R, J))
    s56[:, idx3] = e56
    e57 = he2 * (-1.0) * c0 * h1[:, idx2] / np.square(np.square(h1[:, idx2] + h1[:, idx3] + f64(reserve))) * (-1.0) * (h1[:, idx2] + h1[:, idx3] + f64(reserve)) * 2.0
    s57 = np.zeros((R, J))
    s57[:, idx3] = e57
    e58 = he1 * c0 / np.square(h1[:, idx2] + h1[:, idx3] + f64(reserve)) * (-1.0)
    s58 = np.zeros((R, J))
    s58[:, idx3] = e58
    hh1 = hda * dh1 + s51 + s52 + s53 + s54 + s55 + s56 + s57 + s58
    ha = hh1 * h1
    y = ha * f64(og) + f64(base)
    return y

@@ -1,0 +1,200 @@
+from contextlib import ExitStack
+
+import concourse.mybir as mybir
+from concourse.masks import make_identity
+
+K, R, F, T, J, M = 512, 128, 512, 2048, 512, 256
+FLOPS = 2 * K * R * J + 2 * F * R * M
+
+F32 = mybir.dt.float32
+BF16 = mybir.dt.bfloat16
+I32 = mybir.dt.int32
+U32 = mybir.dt.uint32
+U16 = mybir.dt.uint16
+U8 = mybir.dt.uint8
+FP8X4 = mybir.dt.float8_e4m3fn_x4
+ALU = mybir.AluOpType
+ACT = mybir.ActivationFunctionType
+
+P = 128
+PACK = 4
+HALF = J // 2
+
+
+def tile_attend_gpratiopairs_kernel(tc, tab_words, tab_scales, w1, reserve, wo, dy, og, base, offs, offs2, offs3, out):
+    nc = tc.nc
+    with ExitStack() as ctx:
+        keep = ctx.enter_context(tc.tile_pool(name="keep", bufs=1))
+        psum = ctx.enter_context(tc.psum_pool(name="psum", bufs=1))
+
+        def sb(name, shape, dtype, tag=""):
+            return keep.tile(shape, dtype, name=name, tag=tag or name, align_bytes=64)
+
+        list1 = sb("list1", [P, J // 16], U16)
+        list2 = sb("list2", [P, M // 16], U16)
+        list3 = sb("list3", [P, M // 16], U16)
+        words = sb("words", [P, T], U32)
+        scales = sb("scales", [P, T], U8)
+        w1_raw = sb("w1_raw", [P, PACK, R], F32)
+        wo_raw = sb("wo_raw", [P, PACK, R], F32)
+        dy_raw = sb("dy_raw", [P, PACK, M], F32)
+        res_col = sb("res_col", [P, 1], F32)
+        og_col = sb("og_col", [P, 1], F32)
+        base_sb = sb("base_sb", [P, J], F32)
+
+        nc.vector.memset(scales[:, : T // 2].bitcast(I32), 0)
+        nc.gpsimd.memset(scales[:, T // 2 :].bitcast(I32), 0)
+        nc.sync.dma_start(list1[:], offs)
+        nc.sync.dma_start(w1_raw[:], w1.rearrange("(p t) r -> p t r", t=PACK))
+        for q in range(4):
+            (nc.sync, nc.scalar)[q % 2].dma_start(scales[32 * q : 32 * q + 4, :].bitcast(I32), tab_scales[0, 4 * q : 4 * q + 4, :].bitcast(I32))
+        nc.sync.dma_start(words[:].bitcast(I32), tab_words[0].rearrange("p n t -> p (n t)").bitcast(I32))
+        nc.scalar.dma_start(res_col[:], reserve)
+        nc.sync.dma_start(list2[:], offs2)
+        nc.sync.dma_start(list3[:], offs3)
+        nc.sync.dma_start(wo_raw[:], wo.rearrange("(p t) r -> p t r", t=PACK))
+        nc.sync.dma_start(dy_raw[:], dy.rearrange("(p t) m -> p t m", t=PACK))
+        nc.sync.dma_start(og_col[:], og)
+        nc.sync.dma_start(base_sb[:], base)
+
+        ident = sb("ident", [P, P], F32)
+        make_identity(nc, ident[:])
+
+        first2 = sb("first2", [P, J], F32)
+        first3 = sb("first3", [P, J], F32)
+        second2 = sb("second2", [P, J], F32)
+        second3 = sb("second3", [P, J], F32)
+        for window in (first2, first3, second2, second3):
+            nc.vector.memset(window[:], 0.0)
+
+        def weave(copy, name, raw, width):
+            woven = sb(name, [P, width, PACK], BF16)
+            copy(
+                woven[:].rearrange("p (c i) t -> p c t i", i=4),
+                raw[:].rearrange("p t (c i) -> p c t i", i=4),
+            )
+            return woven
+
+        def quantize(name, woven, width):
+            codes = sb(name + "_codes", [P, width], U32)
+            plane = sb(name + "_scales", [P, width], U8)
+            nc.vector.quantize_mx(out=codes[:].bitcast(FP8X4), scales=plane[:], in_=woven[:].rearrange("p w t -> p (w t)"))
+            return codes, plane
+
+        w1_woven = weave(nc.vector.tensor_copy, "w1_woven", w1_raw, R)
+        picked_scales = sb("picked_scales", [P, J], U8)
+        nc.vector.tensor_copy(picked_scales[:], scales[:].indirect(list1[:]))
+        w1_codes, w1_scales = quantize("w1", w1_woven, R)
+
+        wo_woven = weave(nc.scalar.copy, "wo_woven", wo_raw, R)
+        h1 = sb("h1", [P, J], F32)
+        for half in range(2):
+            cols = slice(half * HALF, (half + 1) * HALF)
+            picked_words = sb("picked_words%d" % half, [P, HALF], U32)
+            nc.vector.tensor_copy(picked_words[:], words[:].indirect(list1[:, half * 16 : (half + 1) * 16]))
+            a_bank = psum.tile([P, HALF], F32, name="a_bank%d" % half)
+            nc.tensor.matmul_mx(
+                out=a_bank[:],
+                lhsT=w1_codes[:].bitcast(FP8X4),
+                lhsT_scale=w1_scales[:],
+                rhs=picked_words[:].bitcast(FP8X4),
+                rhs_scale=picked_scales[:, cols],
+                start=True,
+                stop=True,
+            )
+            nc.scalar.activation(h1[:, cols], a_bank[:], ACT.Exp)
+
+        wo_codes, wo_scales = quantize("wo", wo_woven, R)
+        dy_woven = weave(nc.vector.tensor_copy, "dy_woven", dy_raw, M)
+
+        u = sb("u", [P, M], F32)
+        v = sb("v", [P, M], F32)
+        nc.vector.tensor_copy(u[:], h1[:].indirect(list2[:]))
+        nc.vector.tensor_copy(v[:], h1[:].indirect(list3[:]))
+        dy_codes, dy_scales = quantize("dy", dy_woven, M)
+        c0 = psum.tile([P, M], F32, name="c0")
+        nc.tensor.matmul_mx(
+            out=c0[:],
+            lhsT=wo_codes[:].bitcast(FP8X4),
+            lhsT_scale=wo_scales[:],
+            rhs=dy_codes[:].bitcast(FP8X4),
+            rhs_scale=dy_scales[:],
+            start=True,
+            stop=True,
+        )
+
+        den = sb("den", [P, M], F32)
+        nc.vector.scalar_tensor_tensor(den[:], u[:], res_col[:], v[:], ALU.add, ALU.add)
+        root = sb("root", [P, M], F32)
+        nc.scalar.activation(root[:], den[:], ACT.Abs_reciprocal_sqrt)
+        mag = sb("mag", [P, M], F32)
+        nc.scalar.activation(mag[:], root[:], ACT.Square)
+
+        half_sign = sb("half_sign", [P, M], F32)
+        nc.vector.tensor_scalar(half_sign[:], den[:], 0.0, 0.5, ALU.is_ge, ALU.subtract)
+        cu = sb("cu", [P, M], F32)
+        nc.vector.scalar_tensor_tensor(cu[:], u[:], -2.0, c0[:], ALU.mult, ALU.mult)
+        rec = sb("rec", [P, M], F32)
+        nc.vector.scalar_tensor_tensor(rec[:], mag[:], 2.0, half_sign[:], ALU.mult, ALU.mult)
+
+        shares = sb("shares", [P, 4, M], F32)
+        alpha = sb("alpha", [P, M], F32)
+        beta, delta = shares[:, 1, :], shares[:, 2, :]
+        nc.vector.tensor_tensor(beta, v[:], rec[:], ALU.mult)
+        nc.vector.tensor_tensor(alpha[:], u[:], rec[:], ALU.mult)
+        beta_sq = sb("beta_sq", [P, M], F32)
+        centred_sq = sb("centred_sq", [P, M], F32)
+        mix = sb("mix", [P, M], F32)
+        nc.scalar.activation(beta_sq[:], beta, ACT.Square)
+        nc.scalar.activation(delta, alpha[:], ACT.Copy, bias=-1.0, scale=2.0)
+        nc.scalar.activation(centred_sq[:], delta, ACT.Square)
+        nc.scalar.activation(mix[:], centred_sq[:], ACT.Copy, bias=-0.25, scale=0.25)
+        nc.scalar.activation(shares[:, 0, :], alpha[:], ACT.Copy, bias=-1.0, scale=1.0)
+        nc.scalar.activation(shares[:, 3, :], beta, ACT.Copy, bias=-1.0, scale=2.0)
+
+        cr = sb("cr", [P, M], F32)
+        nc.vector.scalar_tensor_tensor(cr[:], c0[:], og_col[:], rec[:], ALU.mult, ALU.mult)
+
+        nc.vector.tensor_tensor(first3[:].indirect(list3[:]), beta_sq[:], cu[:], ALU.mult)
+        nc.vector.tensor_tensor(first2[:].indirect(list2[:]), mix[:], cu[:], ALU.mult)
+
+        gain2 = sb("gain2", [P, M], F32)
+        gain3 = sb("gain3", [P, M], F32)
+        nc.vector.tensor_tensor(gain2[:], delta, cr[:], ALU.mult)
+        hdh1 = sb("hdh1", [P, J], F32)
+        nc.vector.tensor_tensor(hdh1[:], first2[:], first3[:], ALU.add)
+        nc.vector.tensor_tensor(gain3[:], alpha[:], cr[:], ALU.mult)
+
+        back2 = sb("back2", [P, 1, M], F32)
+        back3 = sb("back3", [P, M], F32)
+        nc.vector.tensor_tensor(back2[:, 0, :], hdh1[:].indirect(list2[:]), gain2[:], ALU.mult)
+        nc.vector.tensor_tensor(back3[:], hdh1[:].indirect(list3[:]), gain3[:], ALU.mult)
+
+        from2 = sb("from2", [P, 2, M], F32)
+        from3 = sb("from3", [P, 2, M], F32)
+        nc.vector.tensor_tensor(from2[:], shares[:, 0:2, :], back2[:].to_broadcast([P, 2, M]), ALU.mult)
+        for n in range(2):
+            nc.vector.tensor_tensor(from3[:, n, :], shares[:, 2 + n, :], back3[:], ALU.mult)
+
+        blocks = (2, 3)
+        turned = [psum.tile([P, P], F32, name="turned%d" % b) for b in blocks]
+        for n, b in enumerate(blocks):
+            nc.tensor.matmul(turned[n][:], base_sb[:, b * P : (b + 1) * P], ident[:], start=True, stop=False, is_transpose=True)
+
+        nc.vector.tensor_tensor(second2[:].indirect(list2[:]), from2[:, 0, :], from3[:, 0, :], ALU.add)
+        nc.vector.tensor_tensor(second3[:].indirect(list3[:]), from2[:, 1, :], from3[:, 1, :], ALU.add)
+
+        partial_high = psum.tile([P, HALF], F32, name="partial_high")
+        turned_sb = [sb("turned_sb%d" % b, [P, P], F32) for b in blocks]
+        for n, b in enumerate(blocks):
+            nc.tensor.matmul(turned[n][:], second2[:, b * P : (b + 1) * P], ident[:], start=False, stop=True, is_transpose=True)
+            nc.scalar.copy(turned_sb[n][:], turned[n][:])
+        for n in range(2):
+            nc.tensor.transpose(partial_high[:, n * P : (n + 1) * P], turned_sb[n][:], ident[:])
+        partial_low = sb("partial_low", [P, HALF], F32)
+        nc.vector.tensor_tensor(partial_low[:], second2[:, :HALF], base_sb[:, :HALF], ALU.add)
+        for half, partial in ((1, partial_high), (0, partial_low)):
+            cols = slice(half * HALF, (half + 1) * HALF)
+            y = sb("y%d" % half, [P, HALF], F32)
+            nc.vector.tensor_tensor(y[:], second3[:, cols], partial[:], ALU.add)
+            (nc.sync, nc.scalar)[half].dma_start(out[:, cols], y[:])

@@ -42,18 +42,17 @@ def tile_attend_gpratiopairs_kernel(tc, tab_words, tab_scales, w1, reserve, wo, 
         og_col = sb("og_col", [P, 1], F32)
         base_sb = sb("base_sb", [P, J], F32)
 
-        nc.vector.memset(scales[:, : T // 2].bitcast(I32), 0)
-        nc.gpsimd.memset(scales[:, T // 2 :].bitcast(I32), 0)
+        nc.vector.memset(scales[:].bitcast(I32), 0)
         nc.sync.dma_start(list1[:], offs)
         nc.sync.dma_start(w1_raw[:], w1.rearrange("(p t) r -> p t r", t=PACK))
         for q in range(4):
             (nc.sync, nc.scalar)[q % 2].dma_start(scales[32 * q : 32 * q + 4, :].bitcast(I32), tab_scales[0, 4 * q : 4 * q + 4, :].bitcast(I32))
         nc.sync.dma_start(words[:].bitcast(I32), tab_words[0].rearrange("p n t -> p (n t)").bitcast(I32))
-        nc.scalar.dma_start(res_col[:], reserve)
-        nc.sync.dma_start(list2[:], offs2)
-        nc.sync.dma_start(list3[:], offs3)
         nc.sync.dma_start(wo_raw[:], wo.rearrange("(p t) r -> p t r", t=PACK))
         nc.sync.dma_start(dy_raw[:], dy.rearrange("(p t) m -> p t m", t=PACK))
+        nc.sync.dma_start(list2[:], offs2)
+        nc.sync.dma_start(list3[:], offs3)
+        nc.sync.dma_start(res_col[:], reserve)
         nc.sync.dma_start(og_col[:], og)
         nc.sync.dma_start(base_sb[:], base)
 
@@ -107,10 +106,6 @@ def tile_attend_gpratiopairs_kernel(tc, tab_words, tab_scales, w1, reserve, wo, 
         wo_codes, wo_scales = quantize("wo", wo_woven, R)
         dy_woven = weave(nc.vector.tensor_copy, "dy_woven", dy_raw, M)
 
-        u = sb("u", [P, M], F32)
-        v = sb("v", [P, M], F32)
-        nc.vector.tensor_copy(u[:], h1[:].indirect(list2[:]))
-        nc.vector.tensor_copy(v[:], h1[:].indirect(list3[:]))
         dy_codes, dy_scales = quantize("dy", dy_woven, M)
         c0 = psum.tile([P, M], F32, name="c0")
         nc.tensor.matmul_mx(
@@ -123,12 +118,20 @@ def tile_attend_gpratiopairs_kernel(tc, tab_words, tab_scales, w1, reserve, wo, 
             stop=True,
         )
 
+        u = sb("u", [P, M], F32)
+        v = sb("v", [P, M], F32)
+        nc.vector.tensor_copy(u[:], h1[:].indirect(list2[:]))
+        pair_halves = [slice(n * M // 2, (n + 1) * M // 2) for n in range(2)]
+        for n, pairs in enumerate(pair_halves):
+            nc.vector.tensor_copy(v[:, pairs], h1[:].indirect(list3[:, n * 8 : (n + 1) * 8]))
         den = sb("den", [P, M], F32)
-        nc.vector.scalar_tensor_tensor(den[:], u[:], res_col[:], v[:], ALU.add, ALU.add)
         root = sb("root", [P, M], F32)
-        nc.scalar.activation(root[:], den[:], ACT.Abs_reciprocal_sqrt)
         mag = sb("mag", [P, M], F32)
-        nc.scalar.activation(mag[:], root[:], ACT.Square)
+        for pairs in pair_halves:
+            nc.vector.scalar_tensor_tensor(den[:, pairs], u[:, pairs], res_col[:], v[:, pairs], ALU.add, ALU.add)
+            nc.scalar.activation(root[:, pairs], den[:, pairs], ACT.Abs_reciprocal_sqrt)
+        for pairs in pair_halves:
+            nc.scalar.activation(mag[:, pairs], root[:, pairs], ACT.Square)
 
         half_sign = sb("half_sign", [P, M], F32)
         nc.vector.tensor_scalar(half_sign[:], den[:], 0.0, 0.5, ALU.is_ge, ALU.subtract)

@@ -57,7 +57,8 @@ def tile_attend_gpratiopairs_kernel(tc, tab_words, tab_scales, w1, reserve, wo, 
         nc.sync.dma_start(base_sb[:], base)
 
         ident = sb("ident", [P, P], F32)
-        make_identity(nc, ident[:])
+        nc.vector.memset(ident[:], 0.0)
+        make_identity(nc, ident[:], nomemset=True)
 
         first2 = sb("first2", [P, J], F32)
         first3 = sb("first3", [P, J], F32)
@@ -66,26 +67,31 @@ def tile_attend_gpratiopairs_kernel(tc, tab_words, tab_scales, w1, reserve, wo, 
         for window in (first2, first3, second2, second3):
             nc.vector.memset(window[:], 0.0)
 
+        minus_half = sb("minus_half", [P, 1], F32)
+        nc.vector.memset(minus_half[:], -0.5)
+
         def weave(copy, name, raw, width):
             woven = sb(name, [P, width, PACK], BF16)
             copy(
                 woven[:].rearrange("p (c i) t -> p c t i", i=4),
-                raw[:].rearrange("p t (c i) -> p c t i", i=4),
+                raw.rearrange("p t (c i) -> p c t i", i=4),
             )
             return woven
 
-        def quantize(name, woven, width):
+        def quantize(name, pieces, width):
             codes = sb(name + "_codes", [P, width], U32)
             plane = sb(name + "_scales", [P, width], U8)
-            nc.vector.quantize_mx(out=codes[:].bitcast(FP8X4), scales=plane[:], in_=woven[:].rearrange("p w t -> p (w t)"))
+            for n, woven in enumerate(pieces):
+                cols = slice(n * R, (n + 1) * R)
+                nc.vector.quantize_mx(out=codes[:, cols].bitcast(FP8X4), scales=plane[:, cols], in_=woven[:].rearrange("p w t -> p (w t)"))
             return codes, plane
 
-        w1_woven = weave(nc.vector.tensor_copy, "w1_woven", w1_raw, R)
+        w1_woven = weave(nc.vector.tensor_copy, "w1_woven", w1_raw[:], R)
         picked_scales = sb("picked_scales", [P, J], U8)
         nc.vector.tensor_copy(picked_scales[:], scales[:].indirect(list1[:]))
-        w1_codes, w1_scales = quantize("w1", w1_woven, R)
+        w1_codes, w1_scales = quantize("w1", [w1_woven], R)
 
-        wo_woven = weave(nc.scalar.copy, "wo_woven", wo_raw, R)
+        wo_woven = weave(nc.scalar.copy, "wo_woven", wo_raw[:], R)
         h1 = sb("h1", [P, J], F32)
         for half in range(2):
             cols = slice(half * HALF, (half + 1) * HALF)
@@ -103,8 +109,9 @@ def tile_attend_gpratiopairs_kernel(tc, tab_words, tab_scales, w1, reserve, wo, 
             )
             nc.scalar.activation(h1[:, cols], a_bank[:], ACT.Exp)
 
-        wo_codes, wo_scales = quantize("wo", wo_woven, R)
-        dy_woven = weave(nc.vector.tensor_copy, "dy_woven", dy_raw, M)
+        wo_codes, wo_scales = quantize("wo", [wo_woven], R)
+        pair_halves = [slice(n * M // 2, (n + 1) * M // 2) for n in range(2)]
+        dy_woven = [weave(nc.vector.tensor_copy, "dy_woven%d" % n, dy_raw[:, :, pairs], M // 2) for n, pairs in enumerate(pair_halves)]
 
         dy_codes, dy_scales = quantize("dy", dy_woven, M)
         c0 = psum.tile([P, M], F32, name="c0")
@@ -121,7 +128,6 @@ def tile_attend_gpratiopairs_kernel(tc, tab_words, tab_scales, w1, reserve, wo, 
         u = sb("u", [P, M], F32)
         v = sb("v", [P, M], F32)
         nc.vector.tensor_copy(u[:], h1[:].indirect(list2[:]))
-        pair_halves = [slice(n * M // 2, (n + 1) * M // 2) for n in range(2)]
         for n, pairs in enumerate(pair_halves):
             nc.vector.tensor_copy(v[:, pairs], h1[:].indirect(list3[:, n * 8 : (n + 1) * 8]))
         den = sb("den", [P, M], F32)
@@ -138,22 +144,24 @@ def tile_attend_gpratiopairs_kernel(tc, tab_words, tab_scales, w1, reserve, wo, 
         cu = sb("cu", [P, M], F32)
         nc.vector.scalar_tensor_tensor(cu[:], u[:], -2.0, c0[:], ALU.mult, ALU.mult)
         rec = sb("rec", [P, M], F32)
-        nc.vector.scalar_tensor_tensor(rec[:], mag[:], 2.0, half_sign[:], ALU.mult, ALU.mult)
+        for pairs in pair_halves:
+            nc.vector.scalar_tensor_tensor(rec[:, pairs], mag[:, pairs], 2.0, half_sign[:, pairs], ALU.mult, ALU.mult)
 
         shares = sb("shares", [P, 4, M], F32)
         alpha = sb("alpha", [P, M], F32)
-        beta, delta = shares[:, 1, :], shares[:, 2, :]
-        nc.vector.tensor_tensor(beta, v[:], rec[:], ALU.mult)
+        beta, centred = shares[:, 1, :], shares[:, 2, :]
+        for pairs in pair_halves:
+            nc.vector.tensor_tensor(shares[:, 1, pairs], v[:, pairs], rec[:, pairs], ALU.mult)
         nc.vector.tensor_tensor(alpha[:], u[:], rec[:], ALU.mult)
         beta_sq = sb("beta_sq", [P, M], F32)
         centred_sq = sb("centred_sq", [P, M], F32)
         mix = sb("mix", [P, M], F32)
         nc.scalar.activation(beta_sq[:], beta, ACT.Square)
-        nc.scalar.activation(delta, alpha[:], ACT.Copy, bias=-1.0, scale=2.0)
-        nc.scalar.activation(centred_sq[:], delta, ACT.Square)
-        nc.scalar.activation(mix[:], centred_sq[:], ACT.Copy, bias=-0.25, scale=0.25)
-        nc.scalar.activation(shares[:, 0, :], alpha[:], ACT.Copy, bias=-1.0, scale=1.0)
-        nc.scalar.activation(shares[:, 3, :], beta, ACT.Copy, bias=-1.0, scale=2.0)
+        nc.scalar.activation(centred_sq[:], alpha[:], ACT.Square, bias=minus_half[:])
+        nc.scalar.activation(mix[:], centred_sq[:], ACT.Copy, bias=-0.25)
+        nc.scalar.activation(centred, alpha[:], ACT.Copy, bias=-0.5)
+        nc.scalar.activation(shares[:, 0, :], alpha[:], ACT.Copy, bias=-1.0)
+        nc.scalar.activation(shares[:, 3, :], beta, ACT.Copy, bias=-0.5)
 
         cr = sb("cr", [P, M], F32)
         nc.vector.scalar_tensor_tensor(cr[:], c0[:], og_col[:], rec[:], ALU.mult, ALU.mult)
@@ -163,10 +171,10 @@ def tile_attend_gpratiopairs_kernel(tc, tab_words, tab_scales, w1, reserve, wo, 
 
         gain2 = sb("gain2", [P, M], F32)
         gain3 = sb("gain3", [P, M], F32)
-        nc.vector.tensor_tensor(gain2[:], delta, cr[:], ALU.mult)
+        nc.vector.scalar_tensor_tensor(gain2[:], centred, 2.0, cr[:], ALU.mult, ALU.mult)
         hdh1 = sb("hdh1", [P, J], F32)
         nc.vector.tensor_tensor(hdh1[:], first2[:], first3[:], ALU.add)
-        nc.vector.tensor_tensor(gain3[:], alpha[:], cr[:], ALU.mult)
+        nc.vector.tensor_tensor(gain3[:], gain2[:], cr[:], ALU.add)
 
         back2 = sb("back2", [P, 1, M], F32)
         back3 = sb("back3", [P, M], F32)
@@ -198,6 +206,6 @@ def tile_attend_gpratiopairs_kernel(tc, tab_words, tab_scales, w1, reserve, wo, 
         nc.vector.tensor_tensor(partial_low[:], second2[:, :HALF], base_sb[:, :HALF], ALU.add)
         for half, partial in ((1, partial_high), (0, partial_low)):
             cols = slice(half * HALF, (half + 1) * HALF)
-            y = sb("y%d" % half, [P, HALF], F32)
+            y = sb("y%d" % half, [P, HALF], F32, tag=("turned_sb3", "y1")[half])
             nc.vector.tensor_tensor(y[:], second3[:, cols], partial[:], ALU.add)
             (nc.sync, nc.scalar)[half].dma_start(out[:, cols], y[:])

from contextlib import ExitStack

import concourse.mybir as mybir
from concourse.masks import make_identity

K, R, F, T, J, M = 512, 128, 512, 2048, 512, 256
FLOPS = 2 * K * R * J + 2 * F * R * M

F32 = mybir.dt.float32
BF16 = mybir.dt.bfloat16
I32 = mybir.dt.int32
U32 = mybir.dt.uint32
U16 = mybir.dt.uint16
U8 = mybir.dt.uint8
FP8X4 = mybir.dt.float8_e4m3fn_x4
ALU = mybir.AluOpType
ACT = mybir.ActivationFunctionType

P = 128
PACK = 4
HALF = J // 2


def tile_attend_gpratiopairs_kernel(tc, tab_words, tab_scales, w1, reserve, wo, dy, og, base, offs, offs2, offs3, out):
    nc = tc.nc
    with ExitStack() as ctx:
        keep = ctx.enter_context(tc.tile_pool(name="keep", bufs=1))
        psum = ctx.enter_context(tc.psum_pool(name="psum", bufs=1))

        def sb(name, shape, dtype, tag=""):
            return keep.tile(shape, dtype, name=name, tag=tag or name, align_bytes=64)

        list1 = sb("list1", [P, J // 16], U16)
        list2 = sb("list2", [P, M // 16], U16)
        list3 = sb("list3", [P, M // 16], U16)
        words = sb("words", [P, T], U32)
        scales = sb("scales", [P, T], U8)
        w1_raw = sb("w1_raw", [P, PACK, R], F32)
        wo_raw = sb("wo_raw", [P, PACK, R], F32)
        dy_raw = sb("dy_raw", [P, PACK, M], F32)
        res_col = sb("res_col", [P, 1], F32)
        og_col = sb("og_col", [P, 1], F32)
        base_sb = sb("base_sb", [P, J], F32)

        nc.vector.memset(scales[:].bitcast(I32), 0)
        nc.sync.dma_start(list1[:], offs)
        nc.sync.dma_start(w1_raw[:], w1.rearrange("(p t) r -> p t r", t=PACK))
        for q in range(4):
            (nc.sync, nc.scalar)[q % 2].dma_start(scales[32 * q : 32 * q + 4, :].bitcast(I32), tab_scales[0, 4 * q : 4 * q + 4, :].bitcast(I32))
        nc.sync.dma_start(words[:].bitcast(I32), tab_words[0].rearrange("p n t -> p (n t)").bitcast(I32))
        nc.sync.dma_start(wo_raw[:], wo.rearrange("(p t) r -> p t r", t=PACK))
        nc.sync.dma_start(dy_raw[:], dy.rearrange("(p t) m -> p t m", t=PACK))
        nc.sync.dma_start(list2[:], offs2)
        nc.sync.dma_start(list3[:], offs3)
        nc.sync.dma_start(res_col[:], reserve)
        nc.sync.dma_start(og_col[:], og)
        nc.sync.dma_start(base_sb[:], base)

        ident = sb("ident", [P, P], F32)
        nc.vector.memset(ident[:], 0.0)
        make_identity(nc, ident[:], nomemset=True)

        first2 = sb("first2", [P, J], F32)
        first3 = sb("first3", [P, J], F32)
        second2 = sb("second2", [P, J], F32)
        second3 = sb("second3", [P, J], F32)
        for window in (first2, first3, second2, second3):
            nc.vector.memset(window[:], 0.0)

        minus_half = sb("minus_half", [P, 1], F32)
        nc.vector.memset(minus_half[:], -0.5)

        def weave(copy, name, raw, width):
            woven = sb(name, [P, width, PACK], BF16)
            copy(
                woven[:].rearrange("p (c i) t -> p c t i", i=4),
                raw.rearrange("p t (c i) -> p c t i", i=4),
            )
            return woven

        def quantize(name, pieces, width):
            codes = sb(name + "_codes", [P, width], U32)
            plane = sb(name + "_scales", [P, width], U8)
            for n, woven in enumerate(pieces):
                cols = slice(n * R, (n + 1) * R)
                nc.vector.quantize_mx(out=codes[:, cols].bitcast(FP8X4), scales=plane[:, cols], in_=woven[:].rearrange("p w t -> p (w t)"))
            return codes, plane

        w1_woven = weave(nc.vector.tensor_copy, "w1_woven", w1_raw[:], R)
        picked_scales = sb("picked_scales", [P, J], U8)
        nc.vector.tensor_copy(picked_scales[:], scales[:].indirect(list1[:]))
        w1_codes, w1_scales = quantize("w1", [w1_woven], R)

        wo_woven = weave(nc.scalar.copy, "wo_woven", wo_raw[:], R)
        h1 = sb("h1", [P, J], F32)
        for half in range(2):
            cols = slice(half * HALF, (half + 1) * HALF)
            picked_words = sb("picked_words%d" % half, [P, HALF], U32)
            nc.vector.tensor_copy(picked_words[:], words[:].indirect(list1[:, half * 16 : (half + 1) * 16]))
            a_bank = psum.tile([P, HALF], F32, name="a_bank%d" % half)
            nc.tensor.matmul_mx(
                out=a_bank[:],
                lhsT=w1_codes[:].bitcast(FP8X4),
                lhsT_scale=w1_scales[:],
                rhs=picked_words[:].bitcast(FP8X4),
                rhs_scale=picked_scales[:, cols],
                start=True,
                stop=True,
            )
            nc.scalar.activation(h1[:, cols], a_bank[:], ACT.Exp)

        wo_codes, wo_scales = quantize("wo", [wo_woven], R)
        pair_halves = [slice(n * M // 2, (n + 1) * M // 2) for n in range(2)]
        dy_woven = [weave(nc.vector.tensor_copy, "dy_woven%d" % n, dy_raw[:, :, pairs], M // 2) for n, pairs in enumerate(pair_halves)]

        dy_codes, dy_scales = quantize("dy", dy_woven, M)
        c0 = psum.tile([P, M], F32, name="c0")
        nc.tensor.matmul_mx(
            out=c0[:],
            lhsT=wo_codes[:].bitcast(FP8X4),
            lhsT_scale=wo_scales[:],
            rhs=dy_codes[:].bitcast(FP8X4),
            rhs_scale=dy_scales[:],
            start=True,
            stop=True,
        )

        u = sb("u", [P, M], F32)
        v = sb("v", [P, M], F32)
        nc.vector.tensor_copy(u[:], h1[:].indirect(list2[:]))
        for n, pairs in enumerate(pair_halves):
            nc.vector.tensor_copy(v[:, pairs], h1[:].indirect(list3[:, n * 8 : (n + 1) * 8]))
        den = sb("den", [P, M], F32)
        root = sb("root", [P, M], F32)
        mag = sb("mag", [P, M], F32)
        for pairs in pair_halves:
            nc.vector.scalar_tensor_tensor(den[:, pairs], u[:, pairs], res_col[:], v[:, pairs], ALU.add, ALU.add)
            nc.scalar.activation(root[:, pairs], den[:, pairs], ACT.Abs_reciprocal_sqrt)
        for pairs in pair_halves:
            nc.scalar.activation(mag[:, pairs], root[:, pairs], ACT.Square)

        half_sign = sb("half_sign", [P, M], F32)
        nc.vector.tensor_scalar(half_sign[:], den[:], 0.0, 0.5, ALU.is_ge, ALU.subtract)
        cu = sb("cu", [P, M], F32)
        nc.vector.scalar_tensor_tensor(cu[:], u[:], -2.0, c0[:], ALU.mult, ALU.mult)
        rec = sb("rec", [P, M], F32)
        for pairs in pair_halves:
            nc.vector.scalar_tensor_tensor(rec[:, pairs], mag[:, pairs], 2.0, half_sign[:, pairs], ALU.mult, ALU.mult)

        shares = sb("shares", [P, 4, M], F32)
        alpha = sb("alpha", [P, M], F32)
        beta, centred = shares[:, 1, :], shares[:, 2, :]
        for pairs in pair_halves:
            nc.vector.tensor_tensor(shares[:, 1, pairs], v[:, pairs], rec[:, pairs], ALU.mult)
        nc.vector.tensor_tensor(alpha[:], u[:], rec[:], ALU.mult)
        beta_sq = sb("beta_sq", [P, M], F32)
        centred_sq = sb("centred_sq", [P, M], F32)
        mix = sb("mix", [P, M], F32)
        nc.scalar.activation(beta_sq[:], beta, ACT.Square)
        nc.scalar.activation(centred_sq[:], alpha[:], ACT.Square, bias=minus_half[:])
        nc.scalar.activation(mix[:], centred_sq[:], ACT.Copy, bias=-0.25)
        nc.scalar.activation(centred, alpha[:], ACT.Copy, bias=-0.5)
        nc.scalar.activation(shares[:, 0, :], alpha[:], ACT.Copy, bias=-1.0)
        nc.scalar.activation(shares[:, 3, :], beta, ACT.Copy, bias=-0.5)

        cr = sb("cr", [P, M], F32)
        nc.vector.scalar_tensor_tensor(cr[:], c0[:], og_col[:], rec[:], ALU.mult, ALU.mult)

        nc.vector.tensor_tensor(first3[:].indirect(list3[:]), beta_sq[:], cu[:], ALU.mult)
        nc.vector.tensor_tensor(first2[:].indirect(list2[:]), mix[:], cu[:], ALU.mult)

        gain2 = sb("gain2", [P, M], F32)
        gain3 = sb("gain3", [P, M], F32)
        nc.vector.scalar_tensor_tensor(gain2[:], centred, 2.0, cr[:], ALU.mult, ALU.mult)
        hdh1 = sb("hdh1", [P, J], F32)
        nc.vector.tensor_tensor(hdh1[:], first2[:], first3[:], ALU.add)
        nc.vector.tensor_tensor(gain3[:], gain2[:], cr[:], ALU.add)

        back2 = sb("back2", [P, 1, M], F32)
        back3 = sb("back3", [P, M], F32)
        nc.vector.tensor_tensor(back2[:, 0, :], hdh1[:].indirect(list2[:]), gain2[:], ALU.mult)
        nc.vector.tensor_tensor(back3[:], hdh1[:].indirect(list3[:]), gain3[:], ALU.mult)

        from2 = sb("from2", [P, 2, M], F32)
        from3 = sb("from3", [P, 2, M], F32)
        nc.vector.tensor_tensor(from2[:], shares[:, 0:2, :], back2[:].to_broadcast([P, 2, M]), ALU.mult)
        for n in range(2):
            nc.vector.tensor_tensor(from3[:, n, :], shares[:, 2 + n, :], back3[:], ALU.mult)

        blocks = (2, 3)
        turned = [psum.tile([P, P], F32, name="turned%d" % b) for b in blocks]
        for n, b in enumerate(blocks):
            nc.tensor.matmul(turned[n][:], base_sb[:, b * P : (b + 1) * P], ident[:], start=True, stop=False, is_transpose=True)

        nc.vector.tensor_tensor(second2[:].indirect(list2[:]), from2[:, 0, :], from3[:, 0, :], ALU.add)
        nc.vector.tensor_tensor(second3[:].indirect(list3[:]), from2[:, 1, :], from3[:, 1, :], ALU.add)

        partial_high = psum.tile([P, HALF], F32, name="partial_high")
        turned_sb = [sb("turned_sb%d" % b, [P, P], F32) for b in blocks]
        for n, b in enumerate(blocks):
            nc.tensor.matmul(turned[n][:], second2[:, b * P : (b + 1) * P], ident[:], start=False, stop=True, is_transpose=True)
            nc.scalar.copy(turned_sb[n][:], turned[n][:])
        for n in range(2):
            nc.tensor.transpose(partial_high[:, n * P : (n + 1) * P], turned_sb[n][:], ident[:])
        partial_low = sb("partial_low", [P, HALF], F32)
        nc.vector.tensor_tensor(partial_low[:], second2[:, :HALF], base_sb[:, :HALF], ALU.add)
        for half, partial in ((1, partial_high), (0, partial_low)):
            cols = slice(half * HALF, (half + 1) * HALF)
            y = sb("y%d" % half, [P, HALF], F32, tag=("turned_sb3", "y1")[half])
            nc.vector.tensor_tensor(y[:], second3[:, cols], partial[:], ALU.add)
            (nc.sync, nc.scalar)[half].dma_start(out[:, cols], y[:])
